import numpy as np
import ml_dtypes

BF16 = ml_dtypes.bfloat16


def bf(x):
    return np.asarray(x, np.float32).astype(BF16)


def f32(x):
    return np.asarray(x, np.float32)


def f64(x):
    return np.asarray(x).astype(np.float64)


def striped(idx):
    return np.tile(idx.reshape(-1, 16).T, (8, 1))


S, K, M, N, D, V = 1024, 256, 256, 768, 4, 192


def setup_inputs():
    return {"table": bf(np.random.standard_normal((K, S))), "w": bf(np.random.standard_normal((K, M)) / np.sqrt(D * K)), "r": f32(np.random.standard_normal((M, V))), "offs": striped(np.random.permutation(np.tile(np.arange(S), 2))[:N])}


def reference(table, w, r, offs):
    idx = offs[:16].T.reshape(-1)
    x = f64(table)[:, idx]
    y = f64(w).T @ sum(x[:, t * V : (t + 1) * V] for t in range(D))
    return y + f64(r)

@@ -1,0 +1,60 @@
+import concourse.mybir as mybir
+
+BF16, F32, U16 = mybir.dt.bfloat16, mybir.dt.float32, mybir.dt.uint16
+
+P = 128
+S = 1024
+K = 256
+M = 256
+D = 4
+V = 192
+K_BLOCKS = K // P
+M_BLOCKS = M // P
+PIECE_COLUMNS = V // 16
+BANK = 512
+WARM_UPS = 4
+
+FLOPS = (D - 1) * K * V + 2 * K * M * V + M * V
+
+
+def tile_gather_matmul_kernel(tc, table, w, r, offs, out):
+    nc = tc.nc
+    table_blocks = table.rearrange("(k p) s -> k p s", p=P)
+    out_blocks = out.rearrange("(m p) v -> m p v", p=P)
+
+    with (
+        tc.tile_pool(name="held", bufs=1) as held,
+        tc.psum_pool(name="psum", bufs=1) as psum,
+    ):
+        offsets = held.tile([P, D * PIECE_COLUMNS], U16, name="offsets")
+        nc.sync.dma_start(offsets[:], offs)
+        windows = [held.tile([P, S], BF16, name=f"window{k}") for k in range(K_BLOCKS)]
+        for k in range(K_BLOCKS):
+            nc.sync.dma_start(windows[k][:], table_blocks[k, :, :])
+
+        weights = held.tile([P, K_BLOCKS, M], BF16, name="weights")
+        nc.scalar.dma_start(weights[:], w.rearrange("(k p) m -> p k m", p=P))
+        own = held.tile([P, M_BLOCKS, V], F32, name="own")
+        nc.scalar.dma_start(own[:], r.rearrange("(m p) v -> p m v", p=P))
+
+        zeros = held.tile([P, BANK], BF16, name="zeros")
+        nc.vector.memset(zeros[:], 0.0)
+        unused = psum.tile([P, BANK], F32, name="unused")
+        for i in range(WARM_UPS):
+            nc.tensor.matmul(unused[:], zeros[:, 0:P], zeros[:], start=True, stop=True)
+
+        banks = [psum.tile([P, V], F32, name=f"bank{m}") for m in range(M_BLOCKS)]
+        for m in range(M_BLOCKS):
+            for k in range(K_BLOCKS):
+                for t in range(D):
+                    piece = offsets[:, t * PIECE_COLUMNS : (t + 1) * PIECE_COLUMNS]
+                    nc.tensor.matmul(
+                        banks[m][:],
+                        weights[:, k, m * P : (m + 1) * P],
+                        windows[k][:].indirect(piece),
+                        start=(k == 0 and t == 0),
+                        stop=(k == K_BLOCKS - 1 and t == D - 1),
+                    )
+            result = held.tile([P, V], F32, name=f"result{m}")
+            nc.vector.tensor_tensor(result[:], banks[m][:], own[:, m, :], mybir.AluOpType.add)
+            nc.sync.dma_start(out_blocks[m, :, :], result[:])

@@ -44,8 +44,8 @@ def tile_gather_matmul_kernel(tc, table, w, r, offs, out):
             nc.tensor.matmul(unused[:], zeros[:, 0:P], zeros[:], start=True, stop=True)
 
         banks = [psum.tile([P, V], F32, name=f"bank{m}") for m in range(M_BLOCKS)]
-        for m in range(M_BLOCKS):
-            for k in range(K_BLOCKS):
+        for k in range(K_BLOCKS):
+            for m in range(M_BLOCKS):
                 for t in range(D):
                     piece = offsets[:, t * PIECE_COLUMNS : (t + 1) * PIECE_COLUMNS]
                     nc.tensor.matmul(
@@ -55,6 +55,7 @@ def tile_gather_matmul_kernel(tc, table, w, r, offs, out):
                         start=(k == 0 and t == 0),
                         stop=(k == K_BLOCKS - 1 and t == D - 1),
                     )
+        for m in range(M_BLOCKS):
             result = held.tile([P, V], F32, name=f"result{m}")
             nc.vector.tensor_tensor(result[:], banks[m][:], own[:, m, :], mybir.AluOpType.add)
             nc.sync.dma_start(out_blocks[m, :, :], result[:])

@@ -26,11 +26,11 @@ def tile_gather_matmul_kernel(tc, table, w, r, offs, out):
         tc.tile_pool(name="held", bufs=1) as held,
         tc.psum_pool(name="psum", bufs=1) as psum,
     ):
+        windows = [held.tile([P, S], BF16, name=f"window{k}") for k in range(K_BLOCKS)]
+        nc.sync.dma_start(windows[0][:], table_blocks[0, :, :])
         offsets = held.tile([P, D * PIECE_COLUMNS], U16, name="offsets")
         nc.sync.dma_start(offsets[:], offs)
-        windows = [held.tile([P, S], BF16, name=f"window{k}") for k in range(K_BLOCKS)]
-        for k in range(K_BLOCKS):
-            nc.sync.dma_start(windows[k][:], table_blocks[k, :, :])
+        nc.sync.dma_start(windows[1][:], table_blocks[1, :, :])
 
         weights = held.tile([P, K_BLOCKS, M], BF16, name="weights")
         nc.scalar.dma_start(weights[:], w.rearrange("(k p) m -> p k m", p=P))

@@ -11,8 +11,6 @@ V = 192
 K_BLOCKS = K // P
 M_BLOCKS = M // P
 PIECE_COLUMNS = V // 16
-BANK = 512
-WARM_UPS = 4
 
 FLOPS = (D - 1) * K * V + 2 * K * M * V + M * V
 
@@ -36,12 +34,6 @@ def tile_gather_matmul_kernel(tc, table, w, r, offs, out):
         nc.scalar.dma_start(weights[:], w.rearrange("(k p) m -> p k m", p=P))
         own = held.tile([P, M_BLOCKS, V], F32, name="own")
         nc.scalar.dma_start(own[:], r.rearrange("(m p) v -> p m v", p=P))
-
-        zeros = held.tile([P, BANK], BF16, name="zeros")
-        nc.vector.memset(zeros[:], 0.0)
-        unused = psum.tile([P, BANK], F32, name="unused")
-        for i in range(WARM_UPS):
-            nc.tensor.matmul(unused[:], zeros[:, 0:P], zeros[:], start=True, stop=True)
 
         banks = [psum.tile([P, V], F32, name=f"bank{m}") for m in range(M_BLOCKS)]
         for k in range(K_BLOCKS):

@@ -24,16 +24,16 @@ def tile_gather_matmul_kernel(tc, table, w, r, offs, out):
         tc.tile_pool(name="held", bufs=1) as held,
         tc.psum_pool(name="psum", bufs=1) as psum,
     ):
+        weights = held.tile([P, K_BLOCKS, M], BF16, name="weights")
+        nc.scalar.dma_start(weights[:], w.rearrange("(k p) m -> p k m", p=P))
+
         windows = [held.tile([P, S], BF16, name=f"window{k}") for k in range(K_BLOCKS)]
         nc.sync.dma_start(windows[0][:], table_blocks[0, :, :])
         offsets = held.tile([P, D * PIECE_COLUMNS], U16, name="offsets")
         nc.sync.dma_start(offsets[:], offs)
         nc.sync.dma_start(windows[1][:], table_blocks[1, :, :])
-
-        weights = held.tile([P, K_BLOCKS, M], BF16, name="weights")
-        nc.scalar.dma_start(weights[:], w.rearrange("(k p) m -> p k m", p=P))
         own = held.tile([P, M_BLOCKS, V], F32, name="own")
-        nc.scalar.dma_start(own[:], r.rearrange("(m p) v -> p m v", p=P))
+        nc.sync.dma_start(own[:], r.rearrange("(m p) v -> p m v", p=P))
 
         banks = [psum.tile([P, V], F32, name=f"bank{m}") for m in range(M_BLOCKS)]
         for k in range(K_BLOCKS):

@@ -11,6 +11,7 @@ V = 192
 K_BLOCKS = K // P
 M_BLOCKS = M // P
 PIECE_COLUMNS = V // 16
+WIDE = 2
 
 FLOPS = (D - 1) * K * V + 2 * K * M * V + M * V
 
@@ -35,19 +36,40 @@ def tile_gather_matmul_kernel(tc, table, w, r, offs, out):
         own = held.tile([P, M_BLOCKS, V], F32, name="own")
         nc.sync.dma_start(own[:], r.rearrange("(m p) v -> p m v", p=P))
 
-        banks = [psum.tile([P, V], F32, name=f"bank{m}") for m in range(M_BLOCKS)]
-        for k in range(K_BLOCKS):
-            for m in range(M_BLOCKS):
-                for t in range(D):
-                    piece = offsets[:, t * PIECE_COLUMNS : (t + 1) * PIECE_COLUMNS]
-                    nc.tensor.matmul(
-                        banks[m][:],
-                        weights[:, k, m * P : (m + 1) * P],
-                        windows[k][:].indirect(piece),
-                        start=(k == 0 and t == 0),
-                        stop=(k == K_BLOCKS - 1 and t == D - 1),
-                    )
+        add = mybir.AluOpType.add
+
+        wide_sums = [psum.tile([P, WIDE * V], F32, name=f"wide_sums{m}") for m in range(M_BLOCKS)]
         for m in range(M_BLOCKS):
+            for pair in range(D // WIDE):
+                pieces = offsets[:, pair * WIDE * PIECE_COLUMNS : (pair + 1) * WIDE * PIECE_COLUMNS]
+                nc.tensor.matmul(
+                    wide_sums[m][:],
+                    weights[:, 0, m * P : (m + 1) * P],
+                    windows[0][:].indirect(pieces),
+                    start=(pair == 0),
+                    stop=(pair == D // WIDE - 1),
+                )
+
+        folded = []
+        for m in range(M_BLOCKS):
+            so_far = own[:, m, :]
+            for half in range(WIDE):
+                fold = held.tile([P, V], F32, name=f"fold{m}_{half}")
+                nc.vector.tensor_tensor(fold[:], wide_sums[m][:, half * V : (half + 1) * V], so_far, add)
+                so_far = fold[:]
+            folded.append(so_far)
+
+        sums = [psum.tile([P, V], F32, name=f"sums{m}") for m in range(M_BLOCKS)]
+        for m in range(M_BLOCKS):
+            for t in range(D):
+                piece = offsets[:, t * PIECE_COLUMNS : (t + 1) * PIECE_COLUMNS]
+                nc.tensor.matmul(
+                    sums[m][:],
+                    weights[:, 1, m * P : (m + 1) * P],
+                    windows[1][:].indirect(piece),
+                    start=(t == 0),
+                    stop=(t == D - 1),
+                )
             result = held.tile([P, V], F32, name=f"result{m}")
-            nc.vector.tensor_tensor(result[:], banks[m][:], own[:, m, :], mybir.AluOpType.add)
+            nc.vector.tensor_tensor(result[:], sums[m][:], folded[m], add)
             nc.sync.dma_start(out_blocks[m, :, :], result[:])

@@ -25,11 +25,11 @@ def tile_gather_matmul_kernel(tc, table, w, r, offs, out):
         tc.tile_pool(name="held", bufs=1) as held,
         tc.psum_pool(name="psum", bufs=1) as psum,
     ):
-        weights = held.tile([P, K_BLOCKS, M], BF16, name="weights")
-        nc.scalar.dma_start(weights[:], w.rearrange("(k p) m -> p k m", p=P))
-
         windows = [held.tile([P, S], BF16, name=f"window{k}") for k in range(K_BLOCKS)]
-        nc.sync.dma_start(windows[0][:], table_blocks[0, :, :])
+        nc.scalar.dma_start(windows[0][:], table_blocks[0, :, :])
+
+        weights = held.tile([P, K_BLOCKS, M], BF16, name="weights")
+        nc.sync.dma_start(weights[:], w.rearrange("(k p) m -> p k m", p=P))
         offsets = held.tile([P, D * PIECE_COLUMNS], U16, name="offsets")
         nc.sync.dma_start(offsets[:], offs)
         nc.sync.dma_start(windows[1][:], table_blocks[1, :, :])

@@ -37,39 +37,42 @@ def tile_gather_matmul_kernel(tc, table, w, r, offs, out):
         nc.sync.dma_start(own[:], r.rearrange("(m p) v -> p m v", p=P))
 
         add = mybir.AluOpType.add
+        last_m = M_BLOCKS - 1
 
+        wide_blocks = [K_BLOCKS, K_BLOCKS - 1]
         wide_sums = [psum.tile([P, WIDE * V], F32, name=f"wide_sums{m}") for m in range(M_BLOCKS)]
-        for m in range(M_BLOCKS):
-            for pair in range(D // WIDE):
-                pieces = offsets[:, pair * WIDE * PIECE_COLUMNS : (pair + 1) * WIDE * PIECE_COLUMNS]
-                nc.tensor.matmul(
-                    wide_sums[m][:],
-                    weights[:, 0, m * P : (m + 1) * P],
-                    windows[0][:].indirect(pieces),
-                    start=(pair == 0),
-                    stop=(pair == D // WIDE - 1),
-                )
+        for k in range(K_BLOCKS):
+            for m in range(M_BLOCKS):
+                if k < wide_blocks[m]:
+                    for pair in range(D // WIDE):
+                        pieces = offsets[:, pair * WIDE * PIECE_COLUMNS : (pair + 1) * WIDE * PIECE_COLUMNS]
+                        nc.tensor.matmul(
+                            wide_sums[m][:],
+                            weights[:, k, m * P : (m + 1) * P],
+                            windows[k][:].indirect(pieces),
+                            start=(k == 0 and pair == 0),
+                            stop=(k == wide_blocks[m] - 1 and pair == D // WIDE - 1),
+                        )
 
-        folded = []
-        for m in range(M_BLOCKS):
-            so_far = own[:, m, :]
+        sums = psum.tile([P, V], F32, name="sums")
+        for t in range(D):
+            piece = offsets[:, t * PIECE_COLUMNS : (t + 1) * PIECE_COLUMNS]
+            nc.tensor.matmul(
+                sums[:],
+                weights[:, K_BLOCKS - 1, last_m * P : (last_m + 1) * P],
+                windows[K_BLOCKS - 1][:].indirect(piece),
+                start=(t == 0),
+                stop=(t == D - 1),
+            )
+
+        folded = [own[:, m, :] for m in range(M_BLOCKS)]
+        for m in reversed(range(M_BLOCKS)):
             for half in range(WIDE):
                 fold = held.tile([P, V], F32, name=f"fold{m}_{half}")
-                nc.vector.tensor_tensor(fold[:], wide_sums[m][:, half * V : (half + 1) * V], so_far, add)
-                so_far = fold[:]
-            folded.append(so_far)
+                nc.vector.tensor_tensor(fold[:], wide_sums[m][:, half * V : (half + 1) * V], folded[m], add)
+                folded[m] = fold[:]
 
-        sums = [psum.tile([P, V], F32, name=f"sums{m}") for m in range(M_BLOCKS)]
-        for m in range(M_BLOCKS):
-            for t in range(D):
-                piece = offsets[:, t * PIECE_COLUMNS : (t + 1) * PIECE_COLUMNS]
-                nc.tensor.matmul(
-                    sums[m][:],
-                    weights[:, 1, m * P : (m + 1) * P],
-                    windows[1][:].indirect(piece),
-                    start=(t == 0),
-                    stop=(t == D - 1),
-                )
-            result = held.tile([P, V], F32, name=f"result{m}")
-            nc.vector.tensor_tensor(result[:], sums[m][:], folded[m], add)
-            nc.sync.dma_start(out_blocks[m, :, :], result[:])
+        nc.sync.dma_start(out_blocks[0, :, :], folded[0])
+        result = held.tile([P, V], F32, name="result")
+        nc.vector.tensor_tensor(result[:], sums[:], folded[last_m], add)
+        nc.sync.dma_start(out_blocks[last_m, :, :], result[:])

@@ -11,6 +11,7 @@ V = 192
 K_BLOCKS = K // P
 M_BLOCKS = M // P
 PIECE_COLUMNS = V // 16
+LINE = 256
 WIDE = 2
 
 FLOPS = (D - 1) * K * V + 2 * K * M * V + M * V
@@ -25,15 +26,15 @@ def tile_gather_matmul_kernel(tc, table, w, r, offs, out):
         tc.tile_pool(name="held", bufs=1) as held,
         tc.psum_pool(name="psum", bufs=1) as psum,
     ):
-        windows = [held.tile([P, S], BF16, name=f"window{k}") for k in range(K_BLOCKS)]
+        windows = [held.tile([P, S], BF16, name=f"window{k}", align_bytes=LINE) for k in range(K_BLOCKS)]
         nc.scalar.dma_start(windows[0][:], table_blocks[0, :, :])
 
-        weights = held.tile([P, K_BLOCKS, M], BF16, name="weights")
+        weights = held.tile([P, K_BLOCKS, M], BF16, name="weights", align_bytes=LINE)
         nc.sync.dma_start(weights[:], w.rearrange("(k p) m -> p k m", p=P))
         offsets = held.tile([P, D * PIECE_COLUMNS], U16, name="offsets")
         nc.sync.dma_start(offsets[:], offs)
         nc.sync.dma_start(windows[1][:], table_blocks[1, :, :])
-        own = held.tile([P, M_BLOCKS, V], F32, name="own")
+        own = held.tile([P, M_BLOCKS, V], F32, name="own", align_bytes=LINE)
         nc.sync.dma_start(own[:], r.rearrange("(m p) v -> p m v", p=P))
 
         add = mybir.AluOpType.add
@@ -68,11 +69,11 @@ def tile_gather_matmul_kernel(tc, table, w, r, offs, out):
         folded = [own[:, m, :] for m in range(M_BLOCKS)]
         for m in reversed(range(M_BLOCKS)):
             for half in range(WIDE):
-                fold = held.tile([P, V], F32, name=f"fold{m}_{half}")
+                fold = held.tile([P, V], F32, name=f"fold{m}_{half}", align_bytes=LINE)
                 nc.vector.tensor_tensor(fold[:], wide_sums[m][:, half * V : (half + 1) * V], folded[m], add)
                 folded[m] = fold[:]
 
         nc.sync.dma_start(out_blocks[0, :, :], folded[0])
-        result = held.tile([P, V], F32, name="result")
+        result = held.tile([P, V], F32, name="result", align_bytes=LINE)
         nc.vector.tensor_tensor(result[:], sums[:], folded[last_m], add)
         nc.sync.dma_start(out_blocks[last_m, :, :], result[:])

@@ -20,6 +20,7 @@ FLOPS = (D - 1) * K * V + 2 * K * M * V + M * V
 def tile_gather_matmul_kernel(tc, table, w, r, offs, out):
     nc = tc.nc
     table_blocks = table.rearrange("(k p) s -> k p s", p=P)
+    w_blocks = w.rearrange("(k p) m -> k p m", p=P)
     out_blocks = out.rearrange("(m p) v -> m p v", p=P)
 
     with (
@@ -27,12 +28,12 @@ def tile_gather_matmul_kernel(tc, table, w, r, offs, out):
         tc.psum_pool(name="psum", bufs=1) as psum,
     ):
         windows = [held.tile([P, S], BF16, name=f"window{k}", align_bytes=LINE) for k in range(K_BLOCKS)]
-        nc.scalar.dma_start(windows[0][:], table_blocks[0, :, :])
-
-        weights = held.tile([P, K_BLOCKS, M], BF16, name="weights", align_bytes=LINE)
-        nc.sync.dma_start(weights[:], w.rearrange("(k p) m -> p k m", p=P))
+        weights = [held.tile([P, M], BF16, name=f"weights{k}", align_bytes=LINE) for k in range(K_BLOCKS)]
         offsets = held.tile([P, D * PIECE_COLUMNS], U16, name="offsets")
+        nc.sync.dma_start(windows[0][:], table_blocks[0, :, :])
+        nc.sync.dma_start(weights[0][:], w_blocks[0, :, :])
         nc.sync.dma_start(offsets[:], offs)
+        nc.sync.dma_start(weights[1][:], w_blocks[1, :, :])
         nc.sync.dma_start(windows[1][:], table_blocks[1, :, :])
         own = held.tile([P, M_BLOCKS, V], F32, name="own", align_bytes=LINE)
         nc.sync.dma_start(own[:], r.rearrange("(m p) v -> p m v", p=P))
@@ -49,7 +50,7 @@ def tile_gather_matmul_kernel(tc, table, w, r, offs, out):
                         pieces = offsets[:, pair * WIDE * PIECE_COLUMNS : (pair + 1) * WIDE * PIECE_COLUMNS]
                         nc.tensor.matmul(
                             wide_sums[m][:],
-                            weights[:, k, m * P : (m + 1) * P],
+                            weights[k][:, m * P : (m + 1) * P],
                             windows[k][:].indirect(pieces),
                             start=(k == 0 and pair == 0),
                             stop=(k == wide_blocks[m] - 1 and pair == D // WIDE - 1),
@@ -60,7 +61,7 @@ def tile_gather_matmul_kernel(tc, table, w, r, offs, out):
             piece = offsets[:, t * PIECE_COLUMNS : (t + 1) * PIECE_COLUMNS]
             nc.tensor.matmul(
                 sums[:],
-                weights[:, K_BLOCKS - 1, last_m * P : (last_m + 1) * P],
+                weights[K_BLOCKS - 1][:, last_m * P : (last_m + 1) * P],
                 windows[K_BLOCKS - 1][:].indirect(piece),
                 start=(t == 0),
                 stop=(t == D - 1),

@@ -20,7 +20,6 @@ FLOPS = (D - 1) * K * V + 2 * K * M * V + M * V
 def tile_gather_matmul_kernel(tc, table, w, r, offs, out):
     nc = tc.nc
     table_blocks = table.rearrange("(k p) s -> k p s", p=P)
-    w_blocks = w.rearrange("(k p) m -> k p m", p=P)
     out_blocks = out.rearrange("(m p) v -> m p v", p=P)
 
     with (
@@ -28,12 +27,13 @@ def tile_gather_matmul_kernel(tc, table, w, r, offs, out):
         tc.psum_pool(name="psum", bufs=1) as psum,
     ):
         windows = [held.tile([P, S], BF16, name=f"window{k}", align_bytes=LINE) for k in range(K_BLOCKS)]
-        weights = [held.tile([P, M], BF16, name=f"weights{k}", align_bytes=LINE) for k in range(K_BLOCKS)]
+        first_weights = held.tile([P, P], BF16, name="first_weights", align_bytes=LINE)
+        weights = held.tile([P, K_BLOCKS, M], BF16, name="weights", align_bytes=LINE)
         offsets = held.tile([P, D * PIECE_COLUMNS], U16, name="offsets")
         nc.sync.dma_start(windows[0][:], table_blocks[0, :, :])
-        nc.sync.dma_start(weights[0][:], w_blocks[0, :, :])
+        nc.sync.dma_start(first_weights[:], w[:P, :P])
         nc.sync.dma_start(offsets[:], offs)
-        nc.sync.dma_start(weights[1][:], w_blocks[1, :, :])
+        nc.sync.dma_start(weights[:], w.rearrange("(k p) m -> p k m", p=P))
         nc.sync.dma_start(windows[1][:], table_blocks[1, :, :])
         own = held.tile([P, M_BLOCKS, V], F32, name="own", align_bytes=LINE)
         nc.sync.dma_start(own[:], r.rearrange("(m p) v -> p m v", p=P))
@@ -46,11 +46,12 @@ def tile_gather_matmul_kernel(tc, table, w, r, offs, out):
         for k in range(K_BLOCKS):
             for m in range(M_BLOCKS):
                 if k < wide_blocks[m]:
+                    product_weights = first_weights[:] if k == 0 and m == 0 else weights[:, k, m * P : (m + 1) * P]
                     for pair in range(D // WIDE):
                         pieces = offsets[:, pair * WIDE * PIECE_COLUMNS : (pair + 1) * WIDE * PIECE_COLUMNS]
                         nc.tensor.matmul(
                             wide_sums[m][:],
-                            weights[k][:, m * P : (m + 1) * P],
+                            product_weights,
                             windows[k][:].indirect(pieces),
                             start=(k == 0 and pair == 0),
                             stop=(k == wide_blocks[m] - 1 and pair == D // WIDE - 1),
@@ -61,7 +62,7 @@ def tile_gather_matmul_kernel(tc, table, w, r, offs, out):
             piece = offsets[:, t * PIECE_COLUMNS : (t + 1) * PIECE_COLUMNS]
             nc.tensor.matmul(
                 sums[:],
-                weights[K_BLOCKS - 1][:, last_m * P : (last_m + 1) * P],
+                weights[:, K_BLOCKS - 1, last_m * P : (last_m + 1) * P],
                 windows[K_BLOCKS - 1][:].indirect(piece),
                 start=(t == 0),
                 stop=(t == D - 1),

@@ -19,7 +19,8 @@ FLOPS = (D - 1) * K * V + 2 * K * M * V + M * V
 
 def tile_gather_matmul_kernel(tc, table, w, r, offs, out):
     nc = tc.nc
-    table_blocks = table.rearrange("(k p) s -> k p s", p=P)
+    table_blocks = table.rearrange("(p k) s -> k p s", k=K_BLOCKS)
+    w_blocks = w.rearrange("(p k) m -> k p m", k=K_BLOCKS)
     out_blocks = out.rearrange("(m p) v -> m p v", p=P)
 
     with (
@@ -31,9 +32,9 @@ def tile_gather_matmul_kernel(tc, table, w, r, offs, out):
         weights = held.tile([P, K_BLOCKS, M], BF16, name="weights", align_bytes=LINE)
         offsets = held.tile([P, D * PIECE_COLUMNS], U16, name="offsets")
         nc.sync.dma_start(windows[0][:], table_blocks[0, :, :])
-        nc.sync.dma_start(first_weights[:], w[:P, :P])
+        nc.sync.dma_start(first_weights[:], w_blocks[0, :, :P])
         nc.sync.dma_start(offsets[:], offs)
-        nc.sync.dma_start(weights[:], w.rearrange("(k p) m -> p k m", p=P))
+        nc.sync.dma_start(weights[:], w.rearrange("(p k) m -> p k m", k=K_BLOCKS))
         nc.sync.dma_start(windows[1][:], table_blocks[1, :, :])
         own = held.tile([P, M_BLOCKS, V], F32, name="own", align_bytes=LINE)
         nc.sync.dma_start(own[:], r.rearrange("(m p) v -> p m v", p=P))

@@ -20,7 +20,7 @@ FLOPS = (D - 1) * K * V + 2 * K * M * V + M * V
 def tile_gather_matmul_kernel(tc, table, w, r, offs, out):
     nc = tc.nc
     table_blocks = table.rearrange("(p k) s -> k p s", k=K_BLOCKS)
-    w_blocks = w.rearrange("(p k) m -> k p m", k=K_BLOCKS)
+    w_rows = w.rearrange("(p k) m -> p (k m)", k=K_BLOCKS)
     out_blocks = out.rearrange("(m p) v -> m p v", p=P)
 
     with (
@@ -28,13 +28,12 @@ def tile_gather_matmul_kernel(tc, table, w, r, offs, out):
         tc.psum_pool(name="psum", bufs=1) as psum,
     ):
         windows = [held.tile([P, S], BF16, name=f"window{k}", align_bytes=LINE) for k in range(K_BLOCKS)]
-        first_weights = held.tile([P, P], BF16, name="first_weights", align_bytes=LINE)
-        weights = held.tile([P, K_BLOCKS, M], BF16, name="weights", align_bytes=LINE)
+        weights = held.tile([P, K_BLOCKS * M], BF16, name="weights", align_bytes=LINE)
         offsets = held.tile([P, D * PIECE_COLUMNS], U16, name="offsets")
         nc.sync.dma_start(windows[0][:], table_blocks[0, :, :])
-        nc.sync.dma_start(first_weights[:], w_blocks[0, :, :P])
+        nc.sync.dma_start(weights[:, :P], w_rows[:, :P])
         nc.sync.dma_start(offsets[:], offs)
-        nc.sync.dma_start(weights[:], w.rearrange("(p k) m -> p k m", k=K_BLOCKS))
+        nc.sync.dma_start(weights[:, P:], w_rows[:, P:])
         nc.sync.dma_start(windows[1][:], table_blocks[1, :, :])
         own = held.tile([P, M_BLOCKS, V], F32, name="own", align_bytes=LINE)
         nc.sync.dma_start(own[:], r.rearrange("(m p) v -> p m v", p=P))
@@ -47,12 +46,12 @@ def tile_gather_matmul_kernel(tc, table, w, r, offs, out):
         for k in range(K_BLOCKS):
             for m in range(M_BLOCKS):
                 if k < wide_blocks[m]:
-                    product_weights = first_weights[:] if k == 0 and m == 0 else weights[:, k, m * P : (m + 1) * P]
+                    product = k * M_BLOCKS + m
                     for pair in range(D // WIDE):
                         pieces = offsets[:, pair * WIDE * PIECE_COLUMNS : (pair + 1) * WIDE * PIECE_COLUMNS]
                         nc.tensor.matmul(
                             wide_sums[m][:],
-                            product_weights,
+                            weights[:, product * P : (product + 1) * P],
                             windows[k][:].indirect(pieces),
                             start=(k == 0 and pair == 0),
                             stop=(k == wide_blocks[m] - 1 and pair == D // WIDE - 1),
@@ -63,7 +62,7 @@ def tile_gather_matmul_kernel(tc, table, w, r, offs, out):
             piece = offsets[:, t * PIECE_COLUMNS : (t + 1) * PIECE_COLUMNS]
             nc.tensor.matmul(
                 sums[:],
-                weights[:, K_BLOCKS - 1, last_m * P : (last_m + 1) * P],
+                weights[:, (K_BLOCKS * M_BLOCKS - 1) * P :],
                 windows[K_BLOCKS - 1][:].indirect(piece),
                 start=(t == 0),
                 stop=(t == D - 1),

@@ -44,11 +44,11 @@ def tile_gather_matmul_kernel(tc, table, w, r, offs, out):
         wide_blocks = [K_BLOCKS, K_BLOCKS - 1]
         wide_sums = [psum.tile([P, WIDE * V], F32, name=f"wide_sums{m}") for m in range(M_BLOCKS)]
         for k in range(K_BLOCKS):
-            for m in range(M_BLOCKS):
-                if k < wide_blocks[m]:
-                    product = k * M_BLOCKS + m
-                    for pair in range(D // WIDE):
-                        pieces = offsets[:, pair * WIDE * PIECE_COLUMNS : (pair + 1) * WIDE * PIECE_COLUMNS]
+            for pair in range(D // WIDE):
+                pieces = offsets[:, pair * WIDE * PIECE_COLUMNS : (pair + 1) * WIDE * PIECE_COLUMNS]
+                for m in range(M_BLOCKS):
+                    if k < wide_blocks[m]:
+                        product = k * M_BLOCKS + m
                         nc.tensor.matmul(
                             wide_sums[m][:],
                             weights[:, product * P : (product + 1) * P],

@@ -77,5 +77,5 @@ def tile_gather_matmul_kernel(tc, table, w, r, offs, out):
 
         nc.sync.dma_start(out_blocks[0, :, :], folded[0])
         result = held.tile([P, V], F32, name="result", align_bytes=LINE)
-        nc.vector.tensor_tensor(result[:], sums[:], folded[last_m], add)
+        nc.vector.scalar_tensor_tensor(result[:], sums[:], 1.0, folded[last_m], mybir.AluOpType.mult, add)
         nc.sync.dma_start(out_blocks[last_m, :, :], result[:])

import concourse.mybir as mybir

BF16, F32, U16 = mybir.dt.bfloat16, mybir.dt.float32, mybir.dt.uint16

P = 128
S = 1024
K = 256
M = 256
D = 4
V = 192
K_BLOCKS = K // P
M_BLOCKS = M // P
PIECE_COLUMNS = V // 16
LINE = 256
WIDE = 2

FLOPS = (D - 1) * K * V + 2 * K * M * V + M * V


def tile_gather_matmul_kernel(tc, table, w, r, offs, out):
    nc = tc.nc
    table_blocks = table.rearrange("(p k) s -> k p s", k=K_BLOCKS)
    w_rows = w.rearrange("(p k) m -> p (k m)", k=K_BLOCKS)
    out_blocks = out.rearrange("(m p) v -> m p v", p=P)

    with (
        tc.tile_pool(name="held", bufs=1) as held,
        tc.psum_pool(name="psum", bufs=1) as psum,
    ):
        windows = [held.tile([P, S], BF16, name=f"window{k}", align_bytes=LINE) for k in range(K_BLOCKS)]
        weights = held.tile([P, K_BLOCKS * M], BF16, name="weights", align_bytes=LINE)
        offsets = held.tile([P, D * PIECE_COLUMNS], U16, name="offsets")
        nc.sync.dma_start(windows[0][:], table_blocks[0, :, :])
        nc.sync.dma_start(weights[:, :P], w_rows[:, :P])
        nc.sync.dma_start(offsets[:], offs)
        nc.sync.dma_start(weights[:, P:], w_rows[:, P:])
        nc.sync.dma_start(windows[1][:], table_blocks[1, :, :])
        own = held.tile([P, M_BLOCKS, V], F32, name="own", align_bytes=LINE)
        nc.sync.dma_start(own[:], r.rearrange("(m p) v -> p m v", p=P))

        add = mybir.AluOpType.add
        last_m = M_BLOCKS - 1

        wide_blocks = [K_BLOCKS, K_BLOCKS - 1]
        wide_sums = [psum.tile([P, WIDE * V], F32, name=f"wide_sums{m}") for m in range(M_BLOCKS)]
        for k in range(K_BLOCKS):
            for pair in range(D // WIDE):
                pieces = offsets[:, pair * WIDE * PIECE_COLUMNS : (pair + 1) * WIDE * PIECE_COLUMNS]
                for m in range(M_BLOCKS):
                    if k < wide_blocks[m]:
                        product = k * M_BLOCKS + m
                        nc.tensor.matmul(
                            wide_sums[m][:],
                            weights[:, product * P : (product + 1) * P],
                            windows[k][:].indirect(pieces),
                            start=(k == 0 and pair == 0),
                            stop=(k == wide_blocks[m] - 1 and pair == D // WIDE - 1),
                        )

        sums = psum.tile([P, V], F32, name="sums")
        for t in range(D):
            piece = offsets[:, t * PIECE_COLUMNS : (t + 1) * PIECE_COLUMNS]
            nc.tensor.matmul(
                sums[:],
                weights[:, (K_BLOCKS * M_BLOCKS - 1) * P :],
                windows[K_BLOCKS - 1][:].indirect(piece),
                start=(t == 0),
                stop=(t == D - 1),
            )

        folded = [own[:, m, :] for m in range(M_BLOCKS)]
        for m in reversed(range(M_BLOCKS)):
            for half in range(WIDE):
                fold = held.tile([P, V], F32, name=f"fold{m}_{half}", align_bytes=LINE)
                nc.vector.tensor_tensor(fold[:], wide_sums[m][:, half * V : (half + 1) * V], folded[m], add)
                folded[m] = fold[:]

        nc.sync.dma_start(out_blocks[0, :, :], folded[0])
        result = held.tile([P, V], F32, name="result", align_bytes=LINE)
        nc.vector.scalar_tensor_tensor(result[:], sums[:], 1.0, folded[last_m], mybir.AluOpType.mult, add)
        nc.sync.dma_start(out_blocks[last_m, :, :], result[:])
